import numpy as np
import ml_dtypes


def mxq(x, axis, fmt="e4m3"):
    dtype, down = {"e4m3": (ml_dtypes.float8_e4m3fn, 7), "e5m2": (ml_dtypes.float8_e5m2, 14)}[fmt]
    v = np.moveaxis(np.asarray(x, np.float32).astype(ml_dtypes.bfloat16).astype(np.float64), axis, -1)
    blocks = v.reshape(v.shape[:-1] + (-1, 32))
    amax = np.abs(blocks).max(-1, keepdims=True)
    byte = np.maximum(np.where(amax > 0, np.frexp(amax)[1] - 1 + 127, 0) - down, 1)
    scale = np.exp2(byte - 127.0)
    codes = (blocks / scale).astype(np.float32).astype(dtype).astype(np.float64)
    return np.moveaxis((codes * scale).reshape(v.shape), -1, axis)


WIDE = False


def mx_kscale(k):
    if not WIDE:
        return np.ones(k)
    levels = np.array([10, -10, 5, -5, 0])
    if k % 512:
        return np.exp2(np.random.permutation(np.resize(levels, k // 32))).repeat(32)
    a = np.empty((k // 512, 16))
    for p in range(k // 512):
        a[p, :8] = np.random.permutation(np.resize(levels, 8))
        for g in range(8):
            far = levels[np.abs(levels - a[p, g]) >= 10]
            a[p, g + 8] = far[np.random.randint(len(far))]
    return np.exp2(a.ravel()).repeat(32)


BF16 = ml_dtypes.bfloat16


def bf(x):
    return np.asarray(x, np.float32).astype(BF16)


def f64(x):
    return np.asarray(x).astype(np.float64)


E2M1 = np.array([0.0, 0.5, 1.0, 1.5, 2.0, 3.0, 4.0, 6.0, -0.0, -0.5, -1.0, -1.5, -2.0, -3.0, -4.0, -6.0])


def pack_weight(w, fmt):
    k, n = w.shape
    w = f64(bf(w)).reshape(k // 32, 32, n)
    amax = np.abs(w).max(1)
    if fmt == "e4m3":
        byte = np.frexp(amax)[1] - 1 + 127 - 7
    else:
        mant, ex = np.frexp(amax / 6.0)
        byte = np.where(mant > 0.5, ex, ex - 1) + 127
    byte = np.clip(np.where(amax > 0, byte, 1), 1, 254)
    scaled = (w * np.exp2(127.0 - byte)[:, None, :]).reshape(k, n).astype(np.float32)
    by_word = np.ascontiguousarray(scaled.reshape(k // 512, 128, 4, n).transpose(0, 1, 3, 2))
    if fmt == "e4m3":
        words = by_word.astype(ml_dtypes.float8_e4m3fn).view(np.uint8)
    else:
        c = by_word.astype(ml_dtypes.float4_e2m1fn).view(np.uint8) & 0xF
        words = c[..., 0::2] | (c[..., 1::2] << 4)
    return np.ascontiguousarray(words), np.ascontiguousarray(byte.astype(np.uint8).reshape(k // 512, 16, n))


def unpack_weight(words, scales, fmt):
    g, p, n, _ = words.shape
    if fmt == "e4m3":
        vals = np.ascontiguousarray(words).view(ml_dtypes.float8_e4m3fn).astype(np.float64)
    else:
        nib = np.empty((g, p, n, 4), np.uint8)
        nib[..., 0::2] = words & 0xF
        nib[..., 1::2] = words >> 4
        vals = E2M1[nib]
    vals = vals * np.repeat(np.exp2(scales.astype(np.float64) - 127.0), 8, axis=1)[..., None]
    return vals.transpose(0, 1, 3, 2).reshape(g * 512, n)
def pack4(w):
    words, scales = pack_weight(w, "e2m1")
    return words.reshape(words.shape[0], 128, -1), scales


def unpack4(words, scales):
    return unpack_weight(words.reshape(words.shape[0], 128, -1, 2), scales, "e2m1")


T, E, H, C, P = 512, 2048, 8, 128, 2048


def draw0():
    s, f = mx_kscale(E), mx_kscale(T)
    a = np.exp(2.0 * np.random.standard_normal((H, T, P)))
    a = a / a.sum(1, keepdims=True)
    r = np.exp(0.7 * np.random.standard_normal(T))
    z = 1.0 / (a * r[:, None]).sum(1)
    attn_words, attn_scales = pack4((a * f[:, None]).reshape(H * T, P))
    return {"text": bf(np.random.standard_normal((T, E)) * s),
            "wv": bf(np.random.standard_normal((E, H * C)) / np.sqrt(E) / s[:, None]),
            "reweight": bf(r / f),
            "attn_words": attn_words,
            "attn_scales": attn_scales,
            "renorm": bf(z)}


def core(text, wv, reweight, attn_words, attn_scales, renorm):
    v = mxq(f64(text), 1, "e4m3") @ mxq(f64(wv), 0, "e4m3")
    u = mxq(v * f64(reweight)[:, None], 0, "e4m3")
    u = u.reshape(T, H, C).transpose(1, 0, 2)
    a = unpack4(attn_words, attn_scales).reshape(H, T, P).transpose(0, 2, 1)
    y = a @ u
    return y * f64(renorm)[:, :, None]


def e4m3fn_bytes(y):
    return np.clip(np.asarray(y, np.float64), -448.0, 448.0).astype(np.float32).astype(ml_dtypes.float8_e4m3fn).view(np.uint8)


def e4m3fn_values(b):
    return np.asarray(b, np.uint8).view(ml_dtypes.float8_e4m3fn).astype(np.float64)


def setup_inputs():
    d = draw0()
    x0 = np.asarray(d['wv']).astype(np.float64)
    s = (np.max(np.abs(x0), axis=(1,), keepdims=True) / 448.0).astype(np.float32)
    out = {}
    for k, v in d.items():
        if k == 'wv':
            out['wv_bytes'] = e4m3fn_bytes(x0 / s.astype(np.float64))
            out['wv_scale'] = s
        else:
            out[k] = v
    return out


def reference(text, wv_bytes, wv_scale, reweight, attn_words, attn_scales, renorm):
    return core(text, e4m3fn_values(wv_bytes) * wv_scale.astype(np.float64), reweight, attn_words, attn_scales, renorm)

@@ -1,0 +1,297 @@
+from contextlib import ExitStack
+
+import concourse.mybir as mybir
+from concourse.masks import make_identity
+
+FLOPS = 2 * 512 * 2048 * 1024 + 2 * 8 * 2048 * 512 * 128
+
+F32 = mybir.dt.float32
+BF16 = mybir.dt.bfloat16
+I32 = mybir.dt.int32
+U32 = mybir.dt.uint32
+U8 = mybir.dt.uint8
+FP8 = mybir.dt.float8_e4m3fn
+E4X4 = mybir.dt.float8_e4m3fn_x4
+F4X4 = mybir.dt.float4_e2m1fn_x4
+COPY = mybir.ActivationFunctionType.Copy
+MULT = mybir.AluOpType.mult
+
+P = 128
+T, E, H, C, PIX = 512, 2048, 8, 128, 2048
+D = H * C
+G = E // 512
+GW = 512
+S_TILES = PIX // P
+
+
+def tile_prompt_map_edit_s13_kernel(tc, text, wv_bytes, wv_scale, reweight, attn_words, attn_scales, renorm, out):
+    nc = tc.nc
+    with ExitStack() as ctx:
+        keep = ctx.enter_context(tc.tile_pool(name="keep", bufs=1))
+        work = ctx.enter_context(tc.tile_pool(name="work", bufs=3))
+        psum_v = ctx.enter_context(tc.psum_pool(name="psum_v", bufs=2))
+        psum_y = ctx.enter_context(tc.psum_pool(name="psum_y", bufs=6))
+
+        wscale = keep.tile([P, 4 * G], F32, name="wscale")
+        rw = keep.tile([P, 4], BF16, name="rw")
+        rn_rows = keep.tile([P, P], BF16, name="rn_rows")
+        rn_rows32 = keep.tile([P, P], F32, name="rn_rows32")
+        rn = keep.tile([P, P], F32, name="rn")
+        ident = keep.tile([P, P], F32, name="ident")
+        dummy = keep.tile([P, 2], F32, name="dummy")
+        wv_raw = [keep.tile([P, 4 * D], U8, name="wv_raw%d" % g) for g in range(G)]
+        text_sb = [keep.tile([P, E], BF16, name="text_sb%d" % t) for t in range(4)]
+        text_gr = [keep.tile([P, E], BF16, name="text_gr%d" % t, align_bytes=64) for t in range(4)]
+        text_codes = [keep.tile([P, E // 4], U32, name="text_codes%d" % t, align_bytes=64) for t in range(4)]
+        text_scales = [keep.tile([P, E // 4], U8, name="text_scales%d" % t, align_bytes=64) for t in range(4)]
+        wv_codes = [keep.tile([P, D], U32, name="wv_codes%d" % g, align_bytes=64) for g in range(G)]
+        wv_scales = [keep.tile([P, D], U8, name="wv_scales%d" % g, align_bytes=64) for g in range(G)]
+        a_words = [keep.tile([P, 2 * PIX], U8, name="a_words%d" % h, align_bytes=64) for h in range(H)]
+        a_scales = keep.tile([P, H * PIX], U8, name="a_scales", align_bytes=64)
+        u_codes = [keep.tile([P, C], U32, name="u_codes%d" % h, align_bytes=64) for h in range(H)]
+        u_scales = [keep.tile([P, C], U8, name="u_scales%d" % h, align_bytes=64) for h in range(H)]
+        y_sb = [keep.tile([P, S_TILES, C], F32, name="y_sb%d" % h) for h in range(H)]
+
+        nc.vector.memset(dummy[:], 0.0)
+        nc.scalar.activation(out=dummy[:, 0:1], in_=dummy[:, 1:2], func=COPY)
+        nc.vector.memset(a_scales[:].bitcast(I32), 0)
+        make_identity(nc, ident[:])
+
+        nc.sync.dma_start(
+            out=wscale[:].rearrange("p (g t) -> p g t", t=4),
+            in_=wv_scale.rearrange("(g p t) o -> p g (t o)", p=P, t=4),
+        )
+        text_rows = text.rearrange("(m t) e -> m t e", t=4)
+        for g in range(G):
+            nc.sync.dma_start(
+                out=wv_raw[g][:],
+                in_=wv_bytes[512 * g : 512 * (g + 1), :].rearrange("(p t) n -> p (t n)", t=4),
+            )
+        for t in range(4):
+            nc.sync.dma_start(out=text_sb[t][:], in_=text_rows[:, t, :])
+        nc.sync.dma_start(out=rw[:], in_=reweight.rearrange("(p t) -> p t", t=4))
+        nc.sync.dma_start(out=rn_rows[:], in_=renorm.rearrange("h (s p) -> (h s) p", p=P))
+        scale_rows = attn_scales.bitcast(I32).rearrange("h (q r) n -> r q h n", r=4)
+        a_scales_i = a_scales[:].bitcast(I32).rearrange("p (h n) -> p h n", h=H)
+        for r in range(4):
+            nc.sync.dma_start(out=a_scales_i[r:128:32], in_=scale_rows[r])
+        for h in range(H):
+            nc.sync.dma_start(out=a_words[h][:], in_=attn_words[h])
+
+        wide = {}
+        grouped = {}
+        v_ps = {}
+        u_gr = {}
+        y_ps = {}
+
+        def text_turn(t, engs):
+            words = text_sb[t][:].bitcast(F32)
+            for gp in range(2):
+                bank = psum_y.tile([P, 4, P], F32, name="bank")
+                for gg in range(2):
+                    g = 2 * gp + gg
+                    for u in range(2):
+                        nc.tensor.transpose(bank[:, 2 * gg + u, :], words[:, 256 * g + u : 256 * (g + 1) : 2], ident[:])
+                dst = text_gr[t][:, 1024 * gp : 1024 * (gp + 1)].bitcast(F32).rearrange("p (g m u) -> p g m u", g=2, u=2)
+                src = bank[:].rearrange("p (g u) m -> p g m u", u=2)
+                if engs[gp] == "s":
+                    nc.scalar.copy(out=dst, in_=src)
+                else:
+                    nc.vector.tensor_copy(out=dst, in_=src)
+
+        def text_quant(t):
+            nc.vector.quantize_mx(out=text_codes[t][:].bitcast(E4X4), scales=text_scales[t][:], in_=text_gr[t][:])
+
+        def widen(eng, b, g, t):
+            if (b, g) not in wide:
+                w = work.tile([P, 4, GW], BF16, name="wide", bufs=4)
+                wide[(b, g)] = w
+            src = wv_raw[g][:, D * t + GW * b : D * t + GW * (b + 1)].bitcast(FP8)
+            dst = wide[(b, g)][:, t, :]
+            sc = wscale[:, 4 * g + t : 4 * g + t + 1]
+            if eng == "s":
+                nc.scalar.activation(out=dst, in_=src, func=COPY, scale=sc)
+            else:
+                nc.vector.tensor_scalar(out=dst, in0=src, scalar1=sc, scalar2=None, op0=MULT)
+
+        def interleave(b, g):
+            gr = work.tile([P, 4 * GW], BF16, name="grouped", align_bytes=64, bufs=4)
+            grouped[(b, g)] = gr
+            nc.vector.tensor_copy(
+                out=gr[:].rearrange("p (c i t) -> p c t i", i=4, t=4),
+                in_=wide[(b, g)][:].rearrange("p t (c i) -> p c t i", i=4),
+            )
+
+        def wv_quant(b, g):
+            cols = slice(GW * b, GW * (b + 1))
+            nc.vector.quantize_mx(out=wv_codes[g][:, cols].bitcast(E4X4), scales=wv_scales[g][:, cols], in_=grouped[(b, g)][:])
+
+        def stage1(h):
+            ps = psum_v.tile([P, 4, C], F32, name="v_ps")
+            v_ps[h] = ps
+            for t in range(4):
+                for g in range(G):
+                    nc.tensor.matmul_mx(
+                        out=ps[:, t, :],
+                        lhsT=text_codes[t][:, P * g : P * (g + 1)].bitcast(E4X4),
+                        lhsT_scale=text_scales[t][:, P * g : P * (g + 1)],
+                        rhs=wv_codes[g][:, C * h : C * (h + 1)].bitcast(E4X4),
+                        rhs_scale=wv_scales[g][:, C * h : C * (h + 1)],
+                        start=(g == 0),
+                        stop=(g == G - 1),
+                    )
+
+        def u_evict(h):
+            ug = work.tile([P, 4 * C], BF16, name="u_gr", align_bytes=64)
+            u_gr[h] = ug
+            nc.vector.tensor_tensor(
+                out=ug[:].rearrange("p (n t) -> p n t", t=4),
+                in0=v_ps[h][:].rearrange("p t n -> p n t"),
+                in1=rw[:].unsqueeze(1).to_broadcast([P, C, 4]),
+                op=MULT,
+            )
+
+        def u_quant(h):
+            nc.vector.quantize_mx(out=u_codes[h][:].bitcast(E4X4), scales=u_scales[h][:], in_=u_gr[h][:])
+
+        def stage2(h, b):
+            ps = psum_y.tile([P, 4, C], F32, name="bank")
+            y_ps[(h, b)] = ps
+            for j in range(4):
+                s = 4 * b + j
+                nc.tensor.matmul_mx(
+                    out=ps[:, j, :],
+                    lhsT=a_words[h][:, 2 * P * s : 2 * P * (s + 1)].bitcast(F4X4),
+                    lhsT_scale=a_scales[:, PIX * h + P * s : PIX * h + P * (s + 1)],
+                    rhs=u_codes[h][:].bitcast(E4X4),
+                    rhs_scale=u_scales[h][:],
+                    start=True,
+                    stop=True,
+                )
+
+        def y_evict(eng, h, b):
+            ps = y_ps[(h, b)]
+            col = S_TILES * h + 4 * b
+            if eng == "s":
+                for j in range(4):
+                    nc.scalar.activation(
+                        out=y_sb[h][:, 4 * b + j, :], in_=ps[:, j, :], func=COPY, scale=rn[:, col + j : col + j + 1]
+                    )
+            else:
+                nc.vector.tensor_tensor(
+                    out=y_sb[h][:, 4 * b : 4 * b + 4, :],
+                    in0=ps[:],
+                    in1=rn[:, col : col + 4].unsqueeze(2).to_broadcast([P, 4, C]),
+                    op=MULT,
+                )
+
+        def store(h, b0, b1):
+            nc.sync.dma_start(
+                out=out[h].rearrange("(s p) c -> p s c", p=P)[:, 4 * b0 : 4 * b1, :],
+                in_=y_sb[h][:, 4 * b0 : 4 * b1, :],
+            )
+
+        def widen4(b, g, engs):
+            for t in range(4):
+                widen(engs[t], b, g, t)
+
+        widen4(0, 0, "ssvv")
+        interleave(0, 0)
+        widen4(0, 1, "sssv")
+        wv_quant(0, 0)
+        interleave(0, 1)
+        widen4(0, 2, "sssv")
+        wv_quant(0, 1)
+        interleave(0, 2)
+        widen4(0, 3, "sssv")
+        wv_quant(0, 2)
+        interleave(0, 3)
+        widen(  "s", 1, 0, 0)
+        text_turn(0, "ss")
+        wv_quant(0, 3)
+        text_quant(0)
+        text_turn(1, "ss")
+        text_quant(1)
+        text_turn(2, "ss")
+        widen("v", 1, 0, 1)
+        text_quant(2)
+        text_turn(3, "ss")
+        nc.vector.tensor_copy(out=rn_rows32[:], in_=rn_rows[:])
+        widen("v", 1, 0, 2)
+        text_quant(3)
+        widen("v", 1, 0, 3)
+        rn_ps = psum_v.tile([P, P], F32, name="v_ps")
+        nc.tensor.transpose(rn_ps[:], rn_rows32[:], ident[:])
+        nc.scalar.copy(out=rn[:], in_=rn_ps[:])
+
+        def bank_y(eng, h, b, n=2):
+            stage2(h, b)
+            y_evict(eng, h, b)
+            if n == 1:
+                store(h, b, b + 1)
+            elif b % 2:
+                store(h, b - 1, b + 1)
+
+        stage1(0)
+        stage1(1)
+        widen4(1, 1, "ssss")
+        interleave(1, 0)
+        u_evict(0)
+        wv_quant(1, 0)
+        u_quant(0)
+        u_evict(1)
+        widen4(1, 2, "sssv")
+        bank_y("s", 0, 0)
+        interleave(1, 1)
+        u_quant(1)
+        bank_y("s", 0, 1)
+        stage1(2)
+        bank_y("v", 0, 2)
+        u_evict(2)
+        bank_y("s", 0, 3)
+        wv_quant(1, 1)
+        u_quant(2)
+        bank_y("s", 1, 0)
+        interleave(1, 2)
+        bank_y("s", 1, 1)
+        stage1(3)
+        widen4(1, 3, "ssvv")
+        bank_y("s", 1, 2)
+        u_evict(3)
+        bank_y("v", 1, 3)
+        u_quant(3)
+        wv_quant(1, 2)
+        bank_y("s", 2, 0)
+        bank_y("s", 2, 1)
+        interleave(1, 3)
+        bank_y("s", 2, 2)
+        wv_quant(1, 3)
+        stage1(4)
+        bank_y("v", 2, 3)
+        stage1(5)
+        u_evict(4)
+        bank_y("s", 3, 0)
+        bank_y("s", 3, 1)
+        u_quant(4)
+        u_evict(5)
+        bank_y("v", 3, 2)
+        u_quant(5)
+        bank_y("s", 3, 3)
+        for b in range(4):
+            bank_y("svsv"[b], 4, b)
+        stage1(6)
+        for b in range(2):
+            bank_y("svsv"[b], 5, b)
+        u_evict(6)
+        stage1(7)
+        for b in range(2, 4):
+            bank_y("svsv"[b], 5, b)
+        u_quant(6)
+        u_evict(7)
+        bank_y("s", 6, 0)
+        u_quant(7)
+        bank_y("v", 6, 1)
+        bank_y("s", 6, 2)
+        bank_y("v", 6, 3)
+        for b in range(4):
+            bank_y("svsv"[b], 7, b, 1)

@@ -31,6 +31,7 @@ def tile_prompt_map_edit_s13_kernel(tc, text, wv_bytes, wv_scale, reweight, attn
         work = ctx.enter_context(tc.tile_pool(name="work", bufs=3))
         psum_v = ctx.enter_context(tc.psum_pool(name="psum_v", bufs=2))
         psum_y = ctx.enter_context(tc.psum_pool(name="psum_y", bufs=6))
+        ctx.enter_context(tc.manual_schedule())
 
         wscale = keep.tile([P, 4 * G], F32, name="wscale")
         rw = keep.tile([P, 4], BF16, name="rw")

@@ -29,6 +29,7 @@ def tile_prompt_map_edit_s13_kernel(tc, text, wv_bytes, wv_scale, reweight, attn
     with ExitStack() as ctx:
         keep = ctx.enter_context(tc.tile_pool(name="keep", bufs=1))
         work = ctx.enter_context(tc.tile_pool(name="work", bufs=3))
+        ypool = ctx.enter_context(tc.tile_pool(name="ypool", bufs=6))
         psum_v = ctx.enter_context(tc.psum_pool(name="psum_v", bufs=2))
         psum_y = ctx.enter_context(tc.psum_pool(name="psum_y", bufs=6))
         ctx.enter_context(tc.manual_schedule())
@@ -51,7 +52,9 @@ def tile_prompt_map_edit_s13_kernel(tc, text, wv_bytes, wv_scale, reweight, attn
         a_scales = keep.tile([P, H * PIX], U8, name="a_scales", align_bytes=64)
         u_codes = [keep.tile([P, C], U32, name="u_codes%d" % h, align_bytes=64) for h in range(H)]
         u_scales = [keep.tile([P, C], U8, name="u_scales%d" % h, align_bytes=64) for h in range(H)]
-        y_sb = [keep.tile([P, S_TILES, C], F32, name="y_sb%d" % h) for h in range(H)]
+        y_sb = {}
+        rnt16 = keep.tile([P, 64], BF16, name="rnt16")
+        rnt = keep.tile([P, 64], F32, name="rnt")
 
         nc.vector.memset(dummy[:], 0.0)
         nc.scalar.activation(out=dummy[:, 0:1], in_=dummy[:, 1:2], func=COPY)
@@ -72,6 +75,10 @@ def tile_prompt_map_edit_s13_kernel(tc, text, wv_bytes, wv_scale, reweight, attn
             nc.sync.dma_start(out=text_sb[t][:], in_=text_rows[:, t, :])
         nc.sync.dma_start(out=rw[:], in_=reweight.rearrange("(p t) -> p t", t=4))
         nc.sync.dma_start(out=rn_rows[:], in_=renorm.rearrange("h (s p) -> (h s) p", p=P))
+        nc.sync.dma_start(
+            out=rnt16[:].rearrange("p (h k s) -> p h k s", h=4, k=2),
+            in_=renorm[4:8].rearrange("h (k p s) -> p h k s", k=2, s=8),
+        )
         scale_rows = attn_scales.bitcast(I32).rearrange("h (q r) n -> r q h n", r=4)
         a_scales_i = a_scales[:].bitcast(I32).rearrange("p (h n) -> p h n", h=H)
         for r in range(4):
@@ -171,6 +178,7 @@ def tile_prompt_map_edit_s13_kernel(tc, text, wv_bytes, wv_scale, reweight, attn
                 )
 
         def y_evict(eng, h, b):
+            new_y(h)
             ps = y_ps[(h, b)]
             col = S_TILES * h + 4 * b
             if eng == "s":
@@ -186,6 +194,69 @@ def tile_prompt_map_edit_s13_kernel(tc, text, wv_bytes, wv_scale, reweight, attn
                     op=MULT,
                 )
 
+        yt = {}
+        z_ps = {}
+
+        def new_y(h):
+            if h not in y_sb:
+                y = ypool.tile([P, S_TILES, C], F32, name="y_sb")
+                y_sb[h] = y
+
+        def stage2t(h, k, i):
+            ps = psum_y.tile([P, 512], F32, name="bank")
+            y_ps[(h, k, i)] = ps
+            n0 = 512 * (2 * k + i)
+            nc.tensor.matmul_mx(
+                out=ps[:],
+                lhsT=u_codes[h][:].bitcast(E4X4),
+                lhsT_scale=u_scales[h][:],
+                rhs=a_words[h][:, 2 * n0 : 2 * (n0 + 512)].bitcast(F4X4),
+                rhs_scale=a_scales[:, PIX * h + n0 : PIX * h + n0 + 512],
+                start=True,
+                stop=True,
+            )
+
+        def regroup(eng, h, k, i):
+            if i == 0:
+                y = work.tile([P, 8, P], F32, name="yt")
+                yt[(h, k)] = y
+            dst = yt[(h, k)][:, :, 64 * i : 64 * (i + 1)]
+            src = y_ps[(h, k, i)][:].rearrange("c (p s) -> c s p", s=8)
+            if eng == "s":
+                nc.scalar.copy(out=dst, in_=src)
+            else:
+                nc.vector.tensor_copy(out=dst, in_=src)
+
+        def turn(h, k, q):
+            ps = psum_y.tile([P, 4, C], F32, name="bank")
+            z_ps[(h, k, q)] = ps
+            for j in range(4):
+                nc.tensor.transpose(ps[:, j, :], yt[(h, k)][:, 4 * q + j, :], ident[:])
+
+        def z_evict(eng, h, k, q):
+            ps = z_ps[(h, k, q)]
+            col = 16 * (h - 4) + 8 * k + 4 * q
+            new_y(h)
+            s0 = 8 * k + 4 * q
+            if eng == "s":
+                for j in range(4):
+                    nc.scalar.activation(
+                        out=y_sb[h][:, s0 + j, :], in_=ps[:, j, :], func=COPY, scale=rnt[:, col + j : col + j + 1]
+                    )
+            else:
+                nc.vector.tensor_tensor(
+                    out=y_sb[h][:, s0 : s0 + 4, :],
+                    in0=ps[:],
+                    in1=rnt[:, col : col + 4].unsqueeze(2).to_broadcast([P, 4, C]),
+                    op=MULT,
+                )
+
+        def storet(h, k):
+            nc.sync.dma_start(
+                out=out[h].rearrange("(k p s) c -> p k s c", k=2, s=8)[:, k],
+                in_=y_sb[h][:, 8 * k : 8 * k + 8, :],
+            )
+
         def store(h, b0, b1):
             nc.sync.dma_start(
                 out=out[h].rearrange("(s p) c -> p s c", p=P)[:, 4 * b0 : 4 * b1, :],
@@ -196,31 +267,32 @@ def tile_prompt_map_edit_s13_kernel(tc, text, wv_bytes, wv_scale, reweight, attn
             for t in range(4):
                 widen(engs[t], b, g, t)
 
-        widen4(0, 0, "ssvv")
+        widen4(0, 0, "vsvv")
+        widen("v", 1, 0, 1)
+        widen("s", 1, 0, 0)
+        widen("s", 1, 0, 2)
         interleave(0, 0)
-        widen4(0, 1, "sssv")
+        widen4(0, 1, "vsss")
         wv_quant(0, 0)
         interleave(0, 1)
-        widen4(0, 2, "sssv")
+        widen4(0, 2, "vsss")
         wv_quant(0, 1)
+        widen4(0, 3, "vsss")
         interleave(0, 2)
-        widen4(0, 3, "sssv")
         wv_quant(0, 2)
         interleave(0, 3)
-        widen(  "s", 1, 0, 0)
         text_turn(0, "ss")
-        wv_quant(0, 3)
         text_quant(0)
+        wv_quant(0, 3)
         text_turn(1, "ss")
         text_quant(1)
         text_turn(2, "ss")
-        widen("v", 1, 0, 1)
+        nc.vector.tensor_copy(out=rn_rows32[:], in_=rn_rows[:])
+        nc.vector.tensor_copy(out=rnt[:], in_=rnt16[:])
         text_quant(2)
         text_turn(3, "ss")
-        nc.vector.tensor_copy(out=rn_rows32[:], in_=rn_rows[:])
-        widen("v", 1, 0, 2)
-        text_quant(3)
         widen("v", 1, 0, 3)
+        text_quant(3)
         rn_ps = psum_v.tile([P, P], F32, name="v_ps")
         nc.tensor.transpose(rn_ps[:], rn_rows32[:], ident[:])
         nc.scalar.copy(out=rn[:], in_=rn_ps[:])
@@ -237,62 +309,76 @@ def tile_prompt_map_edit_s13_kernel(tc, text, wv_bytes, wv_scale, reweight, attn
         stage1(1)
         widen4(1, 1, "ssss")
         interleave(1, 0)
+        widen4(1, 2, "vsss")
         u_evict(0)
         wv_quant(1, 0)
         u_quant(0)
         u_evict(1)
-        widen4(1, 2, "sssv")
-        bank_y("s", 0, 0)
+        stage1(2)
         interleave(1, 1)
         u_quant(1)
-        bank_y("s", 0, 1)
-        stage1(2)
-        bank_y("v", 0, 2)
-        u_evict(2)
-        bank_y("s", 0, 3)
         wv_quant(1, 1)
-        u_quant(2)
-        bank_y("s", 1, 0)
+        widen("s", 1, 3, 0)
+        widen("s", 1, 3, 1)
+        for b in range(4):
+            bank_y("s", 0, b)
         interleave(1, 2)
-        bank_y("s", 1, 1)
-        stage1(3)
-        widen4(1, 3, "ssvv")
-        bank_y("s", 1, 2)
-        u_evict(3)
-        bank_y("v", 1, 3)
-        u_quant(3)
+        u_evict(2)
         wv_quant(1, 2)
-        bank_y("s", 2, 0)
-        bank_y("s", 2, 1)
+        u_quant(2)
+        for b in range(4):
+            bank_y("s", 1, b)
+        stage1(3)
+        widen("v", 1, 3, 2)
+        widen("v", 1, 3, 3)
+        u_evict(3)
         interleave(1, 3)
-        bank_y("s", 2, 2)
+        u_quant(3)
         wv_quant(1, 3)
+        for b in range(4):
+            bank_y("ssvv"[b], 2, b)
+        bank_y("s", 3, 0)
+        bank_y("v", 3, 1)
+        bank_y("s", 3, 2)
         stage1(4)
-        bank_y("v", 2, 3)
+        bank_y("s", 3, 3)
         stage1(5)
         u_evict(4)
-        bank_y("s", 3, 0)
-        bank_y("s", 3, 1)
         u_quant(4)
         u_evict(5)
-        bank_y("v", 3, 2)
+
+        units = [(h, k) for h in range(4, 8) for k in range(2)]
+
+        def front(n):
+            h, k = units[n]
+            for i in range(2):
+                stage2t(h, k, i)
+                regroup("sv"[i], h, k, i)
+
+        def back(n):
+            h, k = units[n]
+            for q in range(2):
+                turn(h, k, q)
+                z_evict("sv"[q], h, k, q)
+            storet(h, k)
+
+        front(0)
         u_quant(5)
-        bank_y("s", 3, 3)
-        for b in range(4):
-            bank_y("svsv"[b], 4, b)
+        front(1)
+        back(0)
         stage1(6)
-        for b in range(2):
-            bank_y("svsv"[b], 5, b)
+        front(2)
+        back(1)
         u_evict(6)
         stage1(7)
-        for b in range(2, 4):
-            bank_y("svsv"[b], 5, b)
+        front(3)
+        back(2)
         u_quant(6)
         u_evict(7)
-        bank_y("s", 6, 0)
+        front(4)
         u_quant(7)
-        bank_y("v", 6, 1)
-        bank_y("s", 6, 2)
-        bank_y("v", 6, 3)
-        for b in range(4):
-            bank_y("svsv"[b], 7, b, 1)
+        back(3)
+        for n in range(5, 8):
+            front(n)
+            back(n - 1)
+        back(7)

from contextlib import ExitStack

import concourse.mybir as mybir
from concourse.masks import make_identity

FLOPS = 2 * 512 * 2048 * 1024 + 2 * 8 * 2048 * 512 * 128

F32 = mybir.dt.float32
BF16 = mybir.dt.bfloat16
I32 = mybir.dt.int32
U32 = mybir.dt.uint32
U8 = mybir.dt.uint8
FP8 = mybir.dt.float8_e4m3fn
E4X4 = mybir.dt.float8_e4m3fn_x4
F4X4 = mybir.dt.float4_e2m1fn_x4
COPY = mybir.ActivationFunctionType.Copy
MULT = mybir.AluOpType.mult

P = 128
T, E, H, C, PIX = 512, 2048, 8, 128, 2048
D = H * C
G = E // 512
GW = 512
S_TILES = PIX // P


def tile_prompt_map_edit_s13_kernel(tc, text, wv_bytes, wv_scale, reweight, attn_words, attn_scales, renorm, out):
    nc = tc.nc
    with ExitStack() as ctx:
        keep = ctx.enter_context(tc.tile_pool(name="keep", bufs=1))
        work = ctx.enter_context(tc.tile_pool(name="work", bufs=3))
        ypool = ctx.enter_context(tc.tile_pool(name="ypool", bufs=6))
        psum_v = ctx.enter_context(tc.psum_pool(name="psum_v", bufs=2))
        psum_y = ctx.enter_context(tc.psum_pool(name="psum_y", bufs=6))
        ctx.enter_context(tc.manual_schedule())

        wscale = keep.tile([P, 4 * G], F32, name="wscale")
        rw = keep.tile([P, 4], BF16, name="rw")
        rn_rows = keep.tile([P, P], BF16, name="rn_rows")
        rn_rows32 = keep.tile([P, P], F32, name="rn_rows32")
        rn = keep.tile([P, P], F32, name="rn")
        ident = keep.tile([P, P], F32, name="ident")
        dummy = keep.tile([P, 2], F32, name="dummy")
        wv_raw = [keep.tile([P, 4 * D], U8, name="wv_raw%d" % g) for g in range(G)]
        text_sb = [keep.tile([P, E], BF16, name="text_sb%d" % t) for t in range(4)]
        text_gr = [keep.tile([P, E], BF16, name="text_gr%d" % t, align_bytes=64) for t in range(4)]
        text_codes = [keep.tile([P, E // 4], U32, name="text_codes%d" % t, align_bytes=64) for t in range(4)]
        text_scales = [keep.tile([P, E // 4], U8, name="text_scales%d" % t, align_bytes=64) for t in range(4)]
        wv_codes = [keep.tile([P, D], U32, name="wv_codes%d" % g, align_bytes=64) for g in range(G)]
        wv_scales = [keep.tile([P, D], U8, name="wv_scales%d" % g, align_bytes=64) for g in range(G)]
        a_words = [keep.tile([P, 2 * PIX], U8, name="a_words%d" % h, align_bytes=64) for h in range(H)]
        a_scales = keep.tile([P, H * PIX], U8, name="a_scales", align_bytes=64)
        u_codes = [keep.tile([P, C], U32, name="u_codes%d" % h, align_bytes=64) for h in range(H)]
        u_scales = [keep.tile([P, C], U8, name="u_scales%d" % h, align_bytes=64) for h in range(H)]
        y_sb = {}
        rnt16 = keep.tile([P, 64], BF16, name="rnt16")
        rnt = keep.tile([P, 64], F32, name="rnt")

        nc.vector.memset(dummy[:], 0.0)
        nc.scalar.activation(out=dummy[:, 0:1], in_=dummy[:, 1:2], func=COPY)
        nc.vector.memset(a_scales[:].bitcast(I32), 0)
        make_identity(nc, ident[:])

        nc.sync.dma_start(
            out=wscale[:].rearrange("p (g t) -> p g t", t=4),
            in_=wv_scale.rearrange("(g p t) o -> p g (t o)", p=P, t=4),
        )
        text_rows = text.rearrange("(m t) e -> m t e", t=4)
        for g in range(G):
            nc.sync.dma_start(
                out=wv_raw[g][:],
                in_=wv_bytes[512 * g : 512 * (g + 1), :].rearrange("(p t) n -> p (t n)", t=4),
            )
        for t in range(4):
            nc.sync.dma_start(out=text_sb[t][:], in_=text_rows[:, t, :])
        nc.sync.dma_start(out=rw[:], in_=reweight.rearrange("(p t) -> p t", t=4))
        nc.sync.dma_start(out=rn_rows[:], in_=renorm.rearrange("h (s p) -> (h s) p", p=P))
        nc.sync.dma_start(
            out=rnt16[:].rearrange("p (h k s) -> p h k s", h=4, k=2),
            in_=renorm[4:8].rearrange("h (k p s) -> p h k s", k=2, s=8),
        )
        scale_rows = attn_scales.bitcast(I32).rearrange("h (q r) n -> r q h n", r=4)
        a_scales_i = a_scales[:].bitcast(I32).rearrange("p (h n) -> p h n", h=H)
        for r in range(4):
            nc.sync.dma_start(out=a_scales_i[r:128:32], in_=scale_rows[r])
        for h in range(H):
            nc.sync.dma_start(out=a_words[h][:], in_=attn_words[h])

        wide = {}
        grouped = {}
        v_ps = {}
        u_gr = {}
        y_ps = {}

        def text_turn(t, engs):
            words = text_sb[t][:].bitcast(F32)
            for gp in range(2):
                bank = psum_y.tile([P, 4, P], F32, name="bank")
                for gg in range(2):
                    g = 2 * gp + gg
                    for u in range(2):
                        nc.tensor.transpose(bank[:, 2 * gg + u, :], words[:, 256 * g + u : 256 * (g + 1) : 2], ident[:])
                dst = text_gr[t][:, 1024 * gp : 1024 * (gp + 1)].bitcast(F32).rearrange("p (g m u) -> p g m u", g=2, u=2)
                src = bank[:].rearrange("p (g u) m -> p g m u", u=2)
                if engs[gp] == "s":
                    nc.scalar.copy(out=dst, in_=src)
                else:
                    nc.vector.tensor_copy(out=dst, in_=src)

        def text_quant(t):
            nc.vector.quantize_mx(out=text_codes[t][:].bitcast(E4X4), scales=text_scales[t][:], in_=text_gr[t][:])

        def widen(eng, b, g, t):
            if (b, g) not in wide:
                w = work.tile([P, 4, GW], BF16, name="wide", bufs=4)
                wide[(b, g)] = w
            src = wv_raw[g][:, D * t + GW * b : D * t + GW * (b + 1)].bitcast(FP8)
            dst = wide[(b, g)][:, t, :]
            sc = wscale[:, 4 * g + t : 4 * g + t + 1]
            if eng == "s":
                nc.scalar.activation(out=dst, in_=src, func=COPY, scale=sc)
            else:
                nc.vector.tensor_scalar(out=dst, in0=src, scalar1=sc, scalar2=None, op0=MULT)

        def interleave(b, g):
            gr = work.tile([P, 4 * GW], BF16, name="grouped", align_bytes=64, bufs=4)
            grouped[(b, g)] = gr
            nc.vector.tensor_copy(
                out=gr[:].rearrange("p (c i t) -> p c t i", i=4, t=4),
                in_=wide[(b, g)][:].rearrange("p t (c i) -> p c t i", i=4),
            )

        def wv_quant(b, g):
            cols = slice(GW * b, GW * (b + 1))
            nc.vector.quantize_mx(out=wv_codes[g][:, cols].bitcast(E4X4), scales=wv_scales[g][:, cols], in_=grouped[(b, g)][:])

        def stage1(h):
            ps = psum_v.tile([P, 4, C], F32, name="v_ps")
            v_ps[h] = ps
            for t in range(4):
                for g in range(G):
                    nc.tensor.matmul_mx(
                        out=ps[:, t, :],
                        lhsT=text_codes[t][:, P * g : P * (g + 1)].bitcast(E4X4),
                        lhsT_scale=text_scales[t][:, P * g : P * (g + 1)],
                        rhs=wv_codes[g][:, C * h : C * (h + 1)].bitcast(E4X4),
                        rhs_scale=wv_scales[g][:, C * h : C * (h + 1)],
                        start=(g == 0),
                        stop=(g == G - 1),
                    )

        def u_evict(h):
            ug = work.tile([P, 4 * C], BF16, name="u_gr", align_bytes=64)
            u_gr[h] = ug
            nc.vector.tensor_tensor(
                out=ug[:].rearrange("p (n t) -> p n t", t=4),
                in0=v_ps[h][:].rearrange("p t n -> p n t"),
                in1=rw[:].unsqueeze(1).to_broadcast([P, C, 4]),
                op=MULT,
            )

        def u_quant(h):
            nc.vector.quantize_mx(out=u_codes[h][:].bitcast(E4X4), scales=u_scales[h][:], in_=u_gr[h][:])

        def stage2(h, b):
            ps = psum_y.tile([P, 4, C], F32, name="bank")
            y_ps[(h, b)] = ps
            for j in range(4):
                s = 4 * b + j
                nc.tensor.matmul_mx(
                    out=ps[:, j, :],
                    lhsT=a_words[h][:, 2 * P * s : 2 * P * (s + 1)].bitcast(F4X4),
                    lhsT_scale=a_scales[:, PIX * h + P * s : PIX * h + P * (s + 1)],
                    rhs=u_codes[h][:].bitcast(E4X4),
                    rhs_scale=u_scales[h][:],
                    start=True,
                    stop=True,
                )

        def y_evict(eng, h, b):
            new_y(h)
            ps = y_ps[(h, b)]
            col = S_TILES * h + 4 * b
            if eng == "s":
                for j in range(4):
                    nc.scalar.activation(
                        out=y_sb[h][:, 4 * b + j, :], in_=ps[:, j, :], func=COPY, scale=rn[:, col + j : col + j + 1]
                    )
            else:
                nc.vector.tensor_tensor(
                    out=y_sb[h][:, 4 * b : 4 * b + 4, :],
                    in0=ps[:],
                    in1=rn[:, col : col + 4].unsqueeze(2).to_broadcast([P, 4, C]),
                    op=MULT,
                )

        yt = {}
        z_ps = {}

        def new_y(h):
            if h not in y_sb:
                y = ypool.tile([P, S_TILES, C], F32, name="y_sb")
                y_sb[h] = y

        def stage2t(h, k, i):
            ps = psum_y.tile([P, 512], F32, name="bank")
            y_ps[(h, k, i)] = ps
            n0 = 512 * (2 * k + i)
            nc.tensor.matmul_mx(
                out=ps[:],
                lhsT=u_codes[h][:].bitcast(E4X4),
                lhsT_scale=u_scales[h][:],
                rhs=a_words[h][:, 2 * n0 : 2 * (n0 + 512)].bitcast(F4X4),
                rhs_scale=a_scales[:, PIX * h + n0 : PIX * h + n0 + 512],
                start=True,
                stop=True,
            )

        def regroup(eng, h, k, i):
            if i == 0:
                y = work.tile([P, 8, P], F32, name="yt")
                yt[(h, k)] = y
            dst = yt[(h, k)][:, :, 64 * i : 64 * (i + 1)]
            src = y_ps[(h, k, i)][:].rearrange("c (p s) -> c s p", s=8)
            if eng == "s":
                nc.scalar.copy(out=dst, in_=src)
            else:
                nc.vector.tensor_copy(out=dst, in_=src)

        def turn(h, k, q):
            ps = psum_y.tile([P, 4, C], F32, name="bank")
            z_ps[(h, k, q)] = ps
            for j in range(4):
                nc.tensor.transpose(ps[:, j, :], yt[(h, k)][:, 4 * q + j, :], ident[:])

        def z_evict(eng, h, k, q):
            ps = z_ps[(h, k, q)]
            col = 16 * (h - 4) + 8 * k + 4 * q
            new_y(h)
            s0 = 8 * k + 4 * q
            if eng == "s":
                for j in range(4):
                    nc.scalar.activation(
                        out=y_sb[h][:, s0 + j, :], in_=ps[:, j, :], func=COPY, scale=rnt[:, col + j : col + j + 1]
                    )
            else:
                nc.vector.tensor_tensor(
                    out=y_sb[h][:, s0 : s0 + 4, :],
                    in0=ps[:],
                    in1=rnt[:, col : col + 4].unsqueeze(2).to_broadcast([P, 4, C]),
                    op=MULT,
                )

        def storet(h, k):
            nc.sync.dma_start(
                out=out[h].rearrange("(k p s) c -> p k s c", k=2, s=8)[:, k],
                in_=y_sb[h][:, 8 * k : 8 * k + 8, :],
            )

        def store(h, b0, b1):
            nc.sync.dma_start(
                out=out[h].rearrange("(s p) c -> p s c", p=P)[:, 4 * b0 : 4 * b1, :],
                in_=y_sb[h][:, 4 * b0 : 4 * b1, :],
            )

        def widen4(b, g, engs):
            for t in range(4):
                widen(engs[t], b, g, t)

        widen4(0, 0, "vsvv")
        widen("v", 1, 0, 1)
        widen("s", 1, 0, 0)
        widen("s", 1, 0, 2)
        interleave(0, 0)
        widen4(0, 1, "vsss")
        wv_quant(0, 0)
        interleave(0, 1)
        widen4(0, 2, "vsss")
        wv_quant(0, 1)
        widen4(0, 3, "vsss")
        interleave(0, 2)
        wv_quant(0, 2)
        interleave(0, 3)
        text_turn(0, "ss")
        text_quant(0)
        wv_quant(0, 3)
        text_turn(1, "ss")
        text_quant(1)
        text_turn(2, "ss")
        nc.vector.tensor_copy(out=rn_rows32[:], in_=rn_rows[:])
        nc.vector.tensor_copy(out=rnt[:], in_=rnt16[:])
        text_quant(2)
        text_turn(3, "ss")
        widen("v", 1, 0, 3)
        text_quant(3)
        rn_ps = psum_v.tile([P, P], F32, name="v_ps")
        nc.tensor.transpose(rn_ps[:], rn_rows32[:], ident[:])
        nc.scalar.copy(out=rn[:], in_=rn_ps[:])

        def bank_y(eng, h, b, n=2):
            stage2(h, b)
            y_evict(eng, h, b)
            if n == 1:
                store(h, b, b + 1)
            elif b % 2:
                store(h, b - 1, b + 1)

        stage1(0)
        stage1(1)
        widen4(1, 1, "ssss")
        interleave(1, 0)
        widen4(1, 2, "vsss")
        u_evict(0)
        wv_quant(1, 0)
        u_quant(0)
        u_evict(1)
        stage1(2)
        interleave(1, 1)
        u_quant(1)
        wv_quant(1, 1)
        widen("s", 1, 3, 0)
        widen("s", 1, 3, 1)
        for b in range(4):
            bank_y("s", 0, b)
        interleave(1, 2)
        u_evict(2)
        wv_quant(1, 2)
        u_quant(2)
        for b in range(4):
            bank_y("s", 1, b)
        stage1(3)
        widen("v", 1, 3, 2)
        widen("v", 1, 3, 3)
        u_evict(3)
        interleave(1, 3)
        u_quant(3)
        wv_quant(1, 3)
        for b in range(4):
            bank_y("ssvv"[b], 2, b)
        bank_y("s", 3, 0)
        bank_y("v", 3, 1)
        bank_y("s", 3, 2)
        stage1(4)
        bank_y("s", 3, 3)
        stage1(5)
        u_evict(4)
        u_quant(4)
        u_evict(5)

        units = [(h, k) for h in range(4, 8) for k in range(2)]

        def front(n):
            h, k = units[n]
            for i in range(2):
                stage2t(h, k, i)
                regroup("sv"[i], h, k, i)

        def back(n):
            h, k = units[n]
            for q in range(2):
                turn(h, k, q)
                z_evict("sv"[q], h, k, q)
            storet(h, k)

        front(0)
        u_quant(5)
        front(1)
        back(0)
        stage1(6)
        front(2)
        back(1)
        u_evict(6)
        stage1(7)
        front(3)
        back(2)
        u_quant(6)
        u_evict(7)
        front(4)
        u_quant(7)
        back(3)
        for n in range(5, 8):
            front(n)
            back(n - 1)
        back(7)
